import numpy as np, ml_dtypes
CORES = [66,70,74,78,82,86,90,94,98,102,106,110,114,118,122,126]
N = 16
import mx_ref
NC, G = 128, 4
C = np.float32(0.019)
CNT = [[0,0,20,8,0,4,8,0,28,12,4,4,20,0,20,0],[0,0,8,20,0,8,12,4,16,4,12,8,8,28,0,0],[4,8,0,12,4,12,4,12,0,0,0,8,4,20,0,40],[0,0,0,0,12,28,12,8,24,20,0,0,0,16,4,4],[0,16,0,0,0,8,20,4,8,4,16,4,4,4,40,0],[16,4,4,8,0,0,0,0,4,0,4,52,4,4,24,4],[24,0,4,8,36,0,0,0,0,0,0,12,28,0,4,12],[24,28,16,4,0,16,4,0,0,4,12,0,4,0,4,12],[16,0,12,4,0,0,8,0,0,44,16,8,8,12,0,0],[8,4,0,8,12,28,16,12,0,0,0,4,0,0,12,24],[0,24,4,24,0,0,0,0,16,8,0,4,16,20,8,4],[0,12,28,0,12,0,12,8,0,4,12,0,20,12,0,8],[0,20,8,0,12,12,24,16,8,0,0,20,0,0,0,8],[4,0,4,4,20,8,0,28,12,0,28,4,8,0,4,4],[8,8,8,12,0,0,4,28,12,4,24,0,4,8,0,8],[24,4,12,16,20,4,4,8,0,24,0,0,0,4,8,0]]
OFF = [[sum(c[:e]) for e in range(N + 1)] for c in CNT]
BF = ml_dtypes.bfloat16
def cut(t, i, w=512):
    return t[:, w * i:w * i + w]
def tile(rs):
    return np.stack(rs, axis=2).reshape(128, -1).astype(BF)
def layer(w, X):
    out = []
    for i in range(G):
        for t in range(len(X)):
            p = mx_ref.matmul(mx_ref.quantize(cut(w, len(X) * i + t)), X[t])
            z = p if t == 0 else z + p
        out.append(z)
    return out
def act(Z):
    return [np.maximum(z, 0) * C for z in Z]
def setup_inputs(rng):
    def f(*shape):
        return mx_ref.flush((rng.standard_normal(shape, dtype=np.float32) * np.exp2(rng.integers(-2, 3, shape[:-1] + (1,)))).astype(BF))
    return {"x": f(N, 128, 4 * NC), "w1": f(N, 128, G * 512), "w2": f(N, 128, 512), "s1": f(N, 128, G * 512), "s2": f(N, 128, 512)}
def setup_inputs_blocks(rng):
    d = setup_inputs(rng)
    for k in ("x", "w1", "w2", "s1", "s2"): d[k] = mx_ref.spread(d[k], rng, 4)
    return d
def setup_inputs_wide(rng):
    d = setup_inputs(rng)
    for k in ("x", "w1", "w2", "s1", "s2"): d[k] = mx_ref.flush((d[k].astype(np.float32) * np.exp2(rng.integers(-8, 9, (N, 1, 1))).astype(np.float32)).astype(BF))
    return d
def setup_inputs_zeros(rng):
    d = setup_inputs(rng); v = d["x"].reshape(N, 128, -1, 4).copy()
    v[np.broadcast_to((rng.random((N, 1, v.shape[2], 1)) < 0.33), v.shape)] = 0
    d["x"] = v.reshape(d["x"].shape)
    return d
def reference(x, w1, w2, s1, s2):
    y = np.zeros((N, 128, NC), np.float32)
    for j in range(N):
        y[j] = mx_ref.matmul(mx_ref.quantize(s2[j]), mx_ref.quantize(tile(act(layer(s1[j], [mx_ref.quantize(x[j])])))))
    for e in range(N):
        t = np.concatenate([x[j][:, 4 * OFF[j][e]:4 * OFF[j][e + 1]] for j in range(N)], axis=1)
        p = mx_ref.matmul(mx_ref.quantize(w2[e]), mx_ref.quantize(tile(act(layer(w1[e], [mx_ref.quantize(t)])))))
        c = 0
        for j in range(N):
            a, b = OFF[j][e], OFF[j][e + 1]
            y[j][:, a:b] = y[j][:, a:b] + p[:, c:c + b - a]; c += b - a
    return {"y": y}

@@ -1,0 +1,324 @@
+from concourse.bass import DstId, RemoteDMATransfer
+from concourse.mybir import dt, AluOpType, ActivationFunctionType
+
+NB = 352
+SCALE = 0.019
+SCRATCH = {
+    "xt": ("sbuf", [128, 1024], "bfloat16"),
+    "w1t": ("sbuf", [128, 2048], "bfloat16"),
+    "w2t": ("sbuf", [128, 512], "bfloat16"),
+    "s1t": ("sbuf", [128, 2048], "bfloat16"),
+    "s2t": ("sbuf", [128, 512], "bfloat16"),
+    "xq": ("sbuf", [128, 128], "float8_e4m3fn_x4"),
+    "xs": ("sbuf", [128, 128], "uint8"),
+    "wq": ("sbuf", [128, 640], "float8_e4m3fn_x4"),
+    "ws": ("sbuf", [128, 640], "uint8"),
+    "pq": ("sbuf", [128, 640], "float8_e4m3fn_x4"),
+    "ps": ("sbuf", [128, 640], "uint8"),
+    "sq": ("sbuf", [128, 640], "float8_e4m3fn_x4"),
+    "ss": ("sbuf", [128, 640], "uint8"),
+    "bq": ("sbuf", [128, NB], "float8_e4m3fn_x4"),
+    "bs": ("sbuf", [128, NB], "uint8"),
+    "ho": ("sbuf", [128, 4 * NB], "bfloat16"),
+    "hp": ("sbuf", [128, 4 * NB], "bfloat16"),
+    "hoq": ("sbuf", [128, NB], "float8_e4m3fn_x4"),
+    "hos": ("sbuf", [128, NB], "uint8"),
+    "hpq": ("sbuf", [128, NB], "float8_e4m3fn_x4"),
+    "hps": ("sbuf", [128, NB], "uint8"),
+    "kt": ("sbuf", [128, 512], "bfloat16"),
+    "kq": ("sbuf", [128, 128], "float8_e4m3fn_x4"),
+    "ks": ("sbuf", [128, 128], "uint8"),
+    "ret": ("sbuf", [128, NB], "float32"),
+    "land": ("sbuf", [128, 128], "float32"),
+    "ysb": ("sbuf", [128, 128], "float32"),
+    "z": ("psum", [128, 4096], "float32"),
+}
+RG = 8
+SEMAPHORES = (["lx", "lx2", "xgo", "lwa", "lwb", "lw2", "ls1", "ls2", "qx", "qb", "qw", "qs", "xin", "win", "dl", "wl",
+               "rl", "aov", "aos", "apv", "aps", "qho", "qhp", "po", "pp", "ol", "akv", "aks", "qk", "uu", "pin",
+               "yv", "sy"] + ["zo%d" % i for i in range(4)] + ["zp%d" % i for i in range(4)]
+              + ["zk%d" % i for i in range(4)] + ["r%d" % i for i in range(RG)])
+
+
+def share(n, t):
+    out = [n]
+    while len(out) < t:
+        out.sort(reverse=True)
+        out = [out[0] // 2, out[0] // 2] + out[1:]
+    return sorted(out, reverse=True)
+
+
+def classes(runs, ne):
+    runs = sorted(runs)
+    best = [(0.0, [])]
+    for i in range(1, len(runs) + 1):
+        opts = []
+        for k in range(max(0, i - ne), i):
+            w = runs[i - 1][0]
+            rows = 128.0 / share(ne, i - k)[-1]
+            extra = sum(w - q[0] for q in runs[k:i])
+            opts.append((best[k][0] + 1000.0 + rows * (60.0 + 0.42 * w) + 10.0 * extra, best[k][1] + [(w, runs[k:i])]))
+        best.append(min(opts, key=lambda o: o[0]))
+    return best[-1][1]
+
+
+def make_plan(cores, cnt, topo):
+    n = len(cores)
+    nc = sum(cnt[0])
+    off = [[sum(c[:e]) for e in range(n + 1)] for c in cnt]
+    pair = {}
+    for r in range(n):
+        pair[r] = [q for q in range(n) if topo.chip(cores[q]) == topo.chip(cores[r])]
+    heads = sorted(set(pair[r][0] for r in range(n)))
+    span = {h: (h, pair[h][-1] + 1) for h in heads}
+    owner = {}
+    for j in range(n):
+        for h in heads:
+            owner[j, h] = [q for q in pair[h] if topo.die(cores[q]) == topo.die(cores[j])][0]
+    run = {(j, h): (off[j][span[h][0]], off[j][span[h][1]]) for j in range(n) for h in heads}
+    calls = {}
+    slot = {}
+    fill = [0] * n
+    for j in range(n):
+        home = pair[j][0]
+        rs = [(run[j, h][1] - run[j, h][0], h) for h in heads if h != home and run[j, h][1] > run[j, h][0]]
+        calls[j] = classes(rs, 8)
+        for w, group in calls[j]:
+            for _, h in group:
+                a = min(run[j, h][0], nc - w)
+                slot[j, h] = (fill[owner[j, h]], w, run[j, h][0] - a, a)
+                fill[owner[j, h]] += w
+    return {"off": off, "pair": pair, "heads": heads, "span": span, "owner": owner, "run": run, "calls": calls,
+            "slot": slot, "fill": fill, "nc": nc}
+
+
+def rank_program(g, core, T, topo):
+    rank = T.rank_of(core)
+    if rank is None:
+        return
+    cores, cnt = T.cores, T.tables["CNT"]
+    P = make_plan(cores, cnt, topo)
+    off, nc = P["off"], P["nc"]
+    home = P["pair"][rank][0]
+    partner = [q for q in P["pair"][rank] if q != rank][0]
+    S = T.sem
+    V, A, E, Y = g.vector, g.scalar, g.tensor, g.sync
+    bits = lambda m: [i for i in range(16) if (m >> i) & 1]
+    far = [q for q in range(len(cores)) if q not in P["pair"][rank] and topo.die(cores[q]) == topo.die(core)]
+    for q in far + [partner]:
+        assert topo.may_write(core, cores[q])
+    out_eng = bits(topo.mask(core, cores[far[0]]))
+    in_eng = [e for e in bits(topo.mask(core, cores[partner])) if e not in out_eng]
+    load = {e: 0.0 for e in out_eng}
+
+    def deal(t, width_bytes):
+        left = list(out_eng)
+        lists = []
+        for k in share(len(out_eng), t):
+            pick = sorted(left, key=lambda e: (load[e], e))[:k]
+            left = [e for e in left if e not in pick]
+            for e in pick:
+                load[e] += 128.0 / k * (30.0 + width_bytes / 12.0)
+            lists.append(pick)
+        return lists
+
+    def send(parts, remote_sem, local_sem, width_bytes):
+        masks = [sum(1 << e for e in l) for l in deal(len(parts), width_bytes)]
+        if len(parts) == 1:
+            q, o, i = parts[0]
+            rid, pid, _ = topo.addr(cores[q])
+            g.remote_dma(out_ap=o, in_ap=i, remote_sem=remote_sem, local_sem=local_sem, pid=pid, routing_id=rid,
+                         dma_engine_mask=masks[0])
+        else:
+            tr = []
+            for (q, o, i), m in zip(parts, masks):
+                rid, pid, _ = topo.addr(cores[q])
+                tr.append(RemoteDMATransfer(dst_ids=[DstId(rid=rid, pnc=pid)], dma_engine_mask=m, remote_sem=remote_sem,
+                                            src=i, dst=o))
+            g.remote_dma_fused(tr, local_sem=local_sem)
+        return sum(len(bits(m)) for m in masks)
+
+    def engines_in(groups):
+        out = {}
+        for group in groups:
+            for key, k in zip(group, share(len(out_eng), len(group))):
+                out[key] = out.get(key, 0) + k
+        return out
+
+    def return_groups(r):
+        h = P["pair"][r][0]
+        by = {}
+        for j in range(len(cores)):
+            if (j, h) in P["slot"] and P["owner"][j, h] == r:
+                by.setdefault(P["run"][j, h][1] - P["run"][j, h][0], []).append(j)
+        return [(w, by[w]) for w in sorted(by, key=lambda w: (-len(by[w]), -w))]
+
+    x_arrive = sum(2 * engines_in([[h for _, h in gr] for _, gr in P["calls"][j]]).get(home, 0) for j in far)
+    p_arrive = sum(engines_in([js for _, js in return_groups(r)]).get(rank, 0) for r in far)
+
+    own_a, own_b = P["run"][rank, home]
+    own = own_b - own_a
+    L = P["fill"][rank]
+    start = 128 - own if own + L >= 128 else L
+    n = 128 + L - start
+    assert 128 + L <= NB and n >= 128 and start >= 0
+    window = start < 128
+
+    Y.dma_start(T.xt[:, 512:1024], T.x[:, :]).then_inc(S.lx, 16)
+    Y.sem_inc(S.xgo, 1)
+    Y.dma_start(T.w1t[:, 0:1024], T.w1[:, 0:1024]).then_inc(S.lwa, 16)
+    A.wait_ge(S.xgo, 1)
+    A.dma_start(T.w1t[:, 1024:2048], T.w1[:, 1024:2048]).then_inc(S.lwb, 16)
+    A.dma_start(T.w2t[:, :], T.w2[:, :]).then_inc(S.lw2, 16)
+    again = window and own_b < nc
+    if again:
+        A.dma_start(T.xt[:, 4 * own_b:512], T.x[:, 4 * own_b:512]).then_inc(S.lx2, 16)
+
+    V.wait_ge(S.lx, 16)
+    V.quantize_mx(T.xq[:, :], T.xs[:, :], T.xt[:, 512:1024]).then_inc(S.qx, 1)
+    V.wait_ge(S.lwa, 16)
+    V.quantize_mx(T.wq[:, 0:256], T.ws[:, 0:256], T.w1t[:, 0:1024]).then_inc(S.qw, 1)
+    V.wait_ge(S.lwb, 16)
+    V.quantize_mx(T.wq[:, 256:512], T.ws[:, 256:512], T.w1t[:, 1024:2048]).then_inc(S.qw, 1)
+    V.wait_ge(S.lw2, 16)
+    V.quantize_mx(T.wq[:, 512:640], T.ws[:, 512:640], T.w2t[:, :]).then_inc(S.qw, 1)
+    if window:
+        if again:
+            V.wait_ge(S.lx2, 16)
+        V.quantize_mx(T.bq[:, 0:128], T.bs[:, 0:128], T.xt[:, 4 * own_b:4 * own_b + 512]).then_inc(S.qb, 1)
+
+    g.wait_ge(S.qx, 1)
+    left = 0
+    for scales in (False, True):
+        for w, group in P["calls"][rank]:
+            parts = []
+            for _, h in group:
+                s0, _, _, a = P["slot"][rank, h]
+                d = 128 + s0
+                if scales:
+                    parts.append((P["owner"][rank, h], T.bs[:, d:d + w], T.xs[:, a:a + w]))
+                else:
+                    parts.append((P["owner"][rank, h], T.bq[:, d:d + w].bitcast(dt.uint8),
+                                  T.xq[:, a:a + w].bitcast(dt.uint8)))
+            left += send(parts, S.xin, S.dl, w if scales else 4 * w)
+    g.wait_ge(S.qw, 3)
+    rid, pid, _ = topo.addr(cores[partner])
+    m = sum(1 << e for e in in_eng)
+    g.remote_dma(out_ap=T.pq[:, :].bitcast(dt.uint8), in_ap=T.wq[:, :].bitcast(dt.uint8), remote_sem=S.win,
+                 local_sem=S.wl, pid=pid, routing_id=rid, dma_engine_mask=m)
+    g.remote_dma(out_ap=T.ps[:, :], in_ap=T.ws[:, :], remote_sem=S.win, local_sem=S.wl, pid=pid, routing_id=rid,
+                 dma_engine_mask=m)
+
+    Y.wait_ge(S.dl, left)
+    Y.dma_start(T.s1t[:, :], T.s1[:, :]).then_inc(S.ls1, 16)
+    Y.dma_start(T.s2t[:, :], T.s2[:, :]).then_inc(S.ls2, 16)
+
+    bank = lambda b, c=n: T.z[:, 512 * b:512 * b + c]
+    BQ, BS = T.bq[:, start:128 + L], T.bs[:, start:128 + L]
+    order = (0, 2, 1, 3)
+
+    def firsts(wq, ws, name, rq, rs, c, banks):
+        for i in order:
+            E.matmul_mx(bank(banks[i], c), wq[:, 128 * i:128 * i + 128], ws[:, 128 * i:128 * i + 128], rq, rs, True,
+                        True).then_inc(S[name + "%d" % i], 1)
+
+    def acts(dst, name, c, banks, sv, sa):
+        for i in (0, 1):
+            V.wait_ge(S[name + "%d" % i], 1)
+            V.tensor_scalar(dst[:, i:4 * c:4], bank(banks[i], c), 0.0, SCALE, AluOpType.max,
+                            AluOpType.mult).then_inc(sv, 1)
+        for i in (2, 3):
+            A.wait_ge(S[name + "%d" % i], 1)
+            A.activation(dst[:, i:4 * c:4], bank(banks[i], c), ActivationFunctionType.Relu,
+                         scale=SCALE).then_inc(sa, 1)
+
+    OB, PB, KB = (0, 1, 2, 3), (4, 5, 6, 7), (1, 2, 3, 5)
+    E.wait_ge(S.qw, 3)
+    if window:
+        E.wait_ge(S.qb, 1)
+    E.wait_ge(S.xin, x_arrive)
+    firsts(T.wq, T.ws, "zo", BQ, BS, n, OB)
+    E.wait_ge(S.win, 2 * len(in_eng))
+    firsts(T.pq, T.ps, "zp", BQ, BS, n, PB)
+    E.wait_ge(S.qho, 1)
+    E.matmul_mx(bank(0), T.wq[:, 512:640], T.ws[:, 512:640], T.hoq[:, 0:n], T.hos[:, 0:n], True, True).then_inc(S.po, 1)
+    E.wait_ge(S.qhp, 1)
+    E.matmul_mx(bank(4), T.pq[:, 512:640], T.ps[:, 512:640], T.hpq[:, 0:n], T.hps[:, 0:n], True, True).then_inc(S.pp, 1)
+
+    acts(T.ho, "zo", n, OB, S.aov, S.aos)
+    V.wait_ge(S.aov, 2)
+    V.wait_ge(S.aos, 2)
+    V.quantize_mx(T.hoq[:, 0:n], T.hos[:, 0:n], T.ho[:, 0:4 * n]).then_inc(S.qho, 1)
+    acts(T.hp, "zp", n, PB, S.apv, S.aps)
+    V.wait_ge(S.apv, 2)
+    V.wait_ge(S.aps, 2)
+    V.quantize_mx(T.hpq[:, 0:n], T.hps[:, 0:n], T.hp[:, 0:4 * n]).then_inc(S.qhp, 1)
+
+    groups = return_groups(rank)
+    assert len(groups) <= RG
+    jobs = []
+    pos = 0
+    for gi, (w, js) in enumerate(groups):
+        for j in js:
+            jobs.append((j, pos, gi))
+            pos += w
+    need = [0] * len(groups)
+    own_need = 0
+    A.wait_ge(S.po, 1)
+    V.wait_ge(S.pp, 1)
+    for e in (rank, partner):
+        for j, p, gi in jobs + [(rank, None, None)]:
+            c = cnt[j][e]
+            if c == 0:
+                continue
+            lead = off[j][e] - P["run"][j, home][0]
+            if gi is None:
+                src = 128 - own + lead - start
+                dst = T.land[:, off[j][e]:off[j][e] + c]
+                sem = S.ol
+                own_need += 1
+            else:
+                s0, _, skip, _ = P["slot"][j, home]
+                src = 128 + s0 + skip + lead - start
+                dst = T.ret[:, p + lead:p + lead + c]
+                sem = S["r%d" % gi]
+                need[gi] += 1
+            if e == rank:
+                A.activation(dst, T.z[:, src:src + c], ActivationFunctionType.Copy).then_inc(sem, 1)
+            else:
+                V.tensor_copy(dst, T.z[:, 2048 + src:2048 + src + c]).then_inc(sem, 1)
+    back = 0
+    pos = 0
+    for gi, (w, js) in enumerate(groups):
+        g.wait_ge(S["r%d" % gi], need[gi])
+        parts = []
+        for j in js:
+            a, b = P["run"][j, home]
+            parts.append((j, T.land[:, a:b], T.ret[:, pos:pos + w]))
+            pos += w
+        back += send(parts, S.pin, S.rl, 4 * w)
+
+    V.wait_ge(S.ls1, 16)
+    V.quantize_mx(T.sq[:, 0:512], T.ss[:, 0:512], T.s1t[:, :]).then_inc(S.qs, 1)
+    V.wait_ge(S.ls2, 16)
+    V.quantize_mx(T.sq[:, 512:640], T.ss[:, 512:640], T.s2t[:, :]).then_inc(S.qs, 1)
+    E.wait_ge(S.qs, 2)
+    E.wait_ge(S.qx, 1)
+    firsts(T.sq, T.ss, "zk", T.xq[:, :], T.xs[:, :], nc, KB)
+    acts(T.kt, "zk", nc, KB, S.akv, S.aks)
+    V.wait_ge(S.akv, 2)
+    V.wait_ge(S.aks, 2)
+    V.quantize_mx(T.kq[:, :], T.ks[:, :], T.kt[:, :]).then_inc(S.qk, 1)
+    E.wait_ge(S.qk, 1)
+    E.matmul_mx(bank(6, nc), T.sq[:, 512:640], T.ss[:, 512:640], T.kq[:, :], T.ks[:, :], True, True).then_inc(S.uu, 1)
+
+    V.wait_ge(S.uu, 1)
+    if own_need:
+        V.wait_ge(S.ol, own_need)
+    V.wait_ge(S.pin, p_arrive)
+    V.tensor_tensor(T.ysb[:, :], T.land[:, :], bank(6, nc), AluOpType.add).then_inc(S.yv, 1)
+    Y.wait_ge(S.yv, 1)
+    Y.dma_start(T.y[:, :], T.ysb[:, :]).then_inc(S.sy, 16)
+    Y.wait_ge(S.sy, 16)
+    g.wait_ge(S.wl, 2 * len(in_eng))
+    g.wait_ge(S.rl, back)

@@ -34,7 +34,8 @@ SCRATCH = {
     "z": ("psum", [128, 4096], "float32"),
 }
 RG = 8
-SEMAPHORES = (["lx", "lx2", "xgo", "lwa", "lwb", "lw2", "ls1", "ls2", "qx", "qb", "qw", "qs", "xin", "win", "dl", "wl",
+SEMAPHORES = (["lx", "lx2", "xgo", "lwa", "lwb", "lw2", "ls1a", "ls1b", "ls2", "mh", "qx", "qb", "qwa", "qwb", "qw2",
+               "qsa", "qsb", "qs2", "xin", "wina", "winb", "win2", "dl", "wl1", "wl2",
                "rl", "aov", "aos", "apv", "aps", "qho", "qhp", "po", "pp", "ol", "akv", "aks", "qk", "uu", "pin",
                "yv", "sy"] + ["zo%d" % i for i in range(4)] + ["zp%d" % i for i in range(4)]
               + ["zk%d" % i for i in range(4)] + ["r%d" % i for i in range(RG)])
@@ -45,21 +46,42 @@ def share(n, t):
     while len(out) < t:
         out.sort(reverse=True)
         out = [out[0] // 2, out[0] // 2] + out[1:]
-    return sorted(out, reverse=True)
+    return sorted(out)
 
 
-def classes(runs, ne):
+def deal(load, t, cost):
+    lists = []
+    left = sorted(load, key=lambda e: (load[e], e))
+    for k in share(len(left), t):
+        pick = left[:k]
+        left = left[k:]
+        for e in pick:
+            load[e] += cost / k
+        lists.append(pick)
+    return lists
+
+
+def row_cost(width_bytes):
+    return 128.0 * (8.0 + 0.04 * width_bytes)
+
+
+def classes(runs, ne, most=3):
     runs = sorted(runs)
-    best = [(0.0, [])]
-    for i in range(1, len(runs) + 1):
-        opts = []
-        for k in range(max(0, i - ne), i):
-            w = runs[i - 1][0]
-            rows = 128.0 / share(ne, i - k)[-1]
-            extra = sum(w - q[0] for q in runs[k:i])
-            opts.append((best[k][0] + 1000.0 + rows * (60.0 + 0.42 * w) + 10.0 * extra, best[k][1] + [(w, runs[k:i])]))
-        best.append(min(opts, key=lambda o: o[0]))
-    return best[-1][1]
+    best = None
+    m = len(runs)
+    for cuts in range(1 << (m - 1)):
+        edge = [0] + [i + 1 for i in range(m - 1) if (cuts >> i) & 1] + [m]
+        calls = [(runs[b - 1][0], runs[a:b]) for a, b in zip(edge, edge[1:])]
+        if len(calls) > most or max(len(c[1]) for c in calls) > ne:
+            continue
+        load = {e: 0.0 for e in range(ne)}
+        for size in (4, 1):
+            for w, group in calls:
+                deal(load, len(group), row_cost(size * w))
+        cost = max(load.values()) + 10.0 * sum(w - q[0] for w, group in calls for q in group)
+        if best is None or cost < best[0]:
+            best = (cost, calls)
+    return best[1]
 
 
 def make_plan(cores, cnt, topo):
@@ -70,26 +92,47 @@ def make_plan(cores, cnt, topo):
     for r in range(n):
         pair[r] = [q for q in range(n) if topo.chip(cores[q]) == topo.chip(cores[r])]
     heads = sorted(set(pair[r][0] for r in range(n)))
-    span = {h: (h, pair[h][-1] + 1) for h in heads}
     owner = {}
     for j in range(n):
         for h in heads:
             owner[j, h] = [q for q in pair[h] if topo.die(cores[q]) == topo.die(cores[j])][0]
-    run = {(j, h): (off[j][span[h][0]], off[j][span[h][1]]) for j in range(n) for h in heads}
+    run = {(j, h): (off[j][h], off[j][pair[h][-1] + 1]) for j in range(n) for h in heads}
     calls = {}
-    slot = {}
-    fill = [0] * n
+    wide = {}
     for j in range(n):
-        home = pair[j][0]
-        rs = [(run[j, h][1] - run[j, h][0], h) for h in heads if h != home and run[j, h][1] > run[j, h][0]]
+        rs = [(run[j, h][1] - run[j, h][0], h) for h in heads if h != pair[j][0] and run[j, h][1] > run[j, h][0]]
         calls[j] = classes(rs, 8)
         for w, group in calls[j]:
             for _, h in group:
                 a = min(run[j, h][0], nc - w)
-                slot[j, h] = (fill[owner[j, h]], w, run[j, h][0] - a, a)
-                fill[owner[j, h]] += w
-    return {"off": off, "pair": pair, "heads": heads, "span": span, "owner": owner, "run": run, "calls": calls,
-            "slot": slot, "fill": fill, "nc": nc}
+                wide[j, h] = (w, run[j, h][0] - a, a)
+    slot = {}
+    where = {}
+    end = {}
+    for r in range(n):
+        h, o = pair[r]
+        src = [j for j in range(n) if (j, h) in wide and owner[j, h] == r]
+        first = [j for j in src if cnt[j][o] == 0]
+        second = [j for j in src if cnt[j][h] == 0]
+        both = sorted([j for j in src if cnt[j][h] and cnt[j][o]], key=lambda j: cnt[j][o] - cnt[j][h])
+        size = lambda g: sum(wide[j, h][0] for j in g)
+        if cnt[r][h] and cnt[r][o]:
+            seq = both + sorted([first, second], key=size)[0] + sorted([first, second], key=size)[1]
+        elif cnt[r][o]:
+            seq = second + both[::-1] + first
+        else:
+            seq = first + both + second
+        pos = 128
+        for e in (h, o):
+            where[r, r, e] = 128 - (run[r, h][1] - off[r][e])
+        for j in seq:
+            slot[j, h] = pos
+            for e in (h, o):
+                where[r, j, e] = pos + wide[j, h][1] + off[j][e] - off[j][h]
+            pos += wide[j, h][0]
+        end[r] = pos
+    return {"off": off, "pair": pair, "owner": owner, "run": run, "calls": calls, "wide": wide, "slot": slot,
+            "where": where, "end": end, "nc": nc}
 
 
 def rank_program(g, core, T, topo):
@@ -109,21 +152,11 @@ def rank_program(g, core, T, topo):
         assert topo.may_write(core, cores[q])
     out_eng = bits(topo.mask(core, cores[far[0]]))
     in_eng = [e for e in bits(topo.mask(core, cores[partner])) if e not in out_eng]
+    assert len(out_eng) == 8
     load = {e: 0.0 for e in out_eng}
 
-    def deal(t, width_bytes):
-        left = list(out_eng)
-        lists = []
-        for k in share(len(out_eng), t):
-            pick = sorted(left, key=lambda e: (load[e], e))[:k]
-            left = [e for e in left if e not in pick]
-            for e in pick:
-                load[e] += 128.0 / k * (30.0 + width_bytes / 12.0)
-            lists.append(pick)
-        return lists
-
     def send(parts, remote_sem, local_sem, width_bytes):
-        masks = [sum(1 << e for e in l) for l in deal(len(parts), width_bytes)]
+        masks = [sum(1 << e for e in l) for l in deal(load, len(parts), row_cost(width_bytes))]
         if len(parts) == 1:
             q, o, i = parts[0]
             rid, pid, _ = topo.addr(cores[q])
@@ -147,22 +180,32 @@ def rank_program(g, core, T, topo):
 
     def return_groups(r):
         h = P["pair"][r][0]
+        other = [q for q in P["pair"][r] if q != r][0]
         by = {}
         for j in range(len(cores)):
             if (j, h) in P["slot"] and P["owner"][j, h] == r:
-                by.setdefault(P["run"][j, h][1] - P["run"][j, h][0], []).append(j)
-        return [(w, by[w]) for w in sorted(by, key=lambda w: (-len(by[w]), -w))]
+                by.setdefault((cnt[j][other] > 0, P["run"][j, h][1] - P["run"][j, h][0]), []).append(j)
+        keys = sorted(by, key=lambda k: (k[0], -len(by[k]), -k[1]))
+        single = [k for k in keys if k[0] and len(by[k]) == 1]
+        if single:
+            keys.remove(single[0])
+            keys.insert(len([k for k in keys if not k[0]]), single[0])
+        return [(k[1], by[k]) for k in keys]
 
     x_arrive = sum(2 * engines_in([[h for _, h in gr] for _, gr in P["calls"][j]]).get(home, 0) for j in far)
     p_arrive = sum(engines_in([js for _, js in return_groups(r)]).get(rank, 0) for r in far)
 
-    own_a, own_b = P["run"][rank, home]
-    own = own_b - own_a
-    L = P["fill"][rank]
-    start = 128 - own if own + L >= 128 else L
-    n = 128 + L - start
-    assert 128 + L <= NB and n >= 128 and start >= 0
-    window = start < 128
+    own_b = P["run"][rank, home][1]
+    end = P["end"][rank]
+    assert end <= NB
+    views = {}
+    for e in (rank, partner):
+        cols = [(P["where"][rank, j, e], cnt[j][e]) for j in range(len(cores)) if (rank, j, e) in P["where"] and cnt[j][e]]
+        lo = min(c for c, _ in cols)
+        hi = max(c + k for c, k in cols)
+        v = lo if lo + 128 <= end else min(lo, end - 128)
+        views[e] = (lo, hi - lo, v, max(128, hi - v))
+    window = min(views[e][2] for e in views) < 128
 
     Y.dma_start(T.xt[:, 512:1024], T.x[:, :]).then_inc(S.lx, 16)
     Y.sem_inc(S.xgo, 1)
@@ -174,14 +217,20 @@ def rank_program(g, core, T, topo):
     if again:
         A.dma_start(T.xt[:, 4 * own_b:512], T.x[:, 4 * own_b:512]).then_inc(S.lx2, 16)
 
+    fills = 0
+    for e, t in ((rank, T.ho), (partner, T.hp)):
+        if views[e][1] < views[e][3]:
+            V.memset(t[:, 0:4 * views[e][3]], 0.0).then_inc(S.mh, 1)
+            fills += 1
+
     V.wait_ge(S.lx, 16)
     V.quantize_mx(T.xq[:, :], T.xs[:, :], T.xt[:, 512:1024]).then_inc(S.qx, 1)
     V.wait_ge(S.lwa, 16)
-    V.quantize_mx(T.wq[:, 0:256], T.ws[:, 0:256], T.w1t[:, 0:1024]).then_inc(S.qw, 1)
+    V.quantize_mx(T.wq[:, 0:256], T.ws[:, 0:256], T.w1t[:, 0:1024]).then_inc(S.qwa, 1)
     V.wait_ge(S.lwb, 16)
-    V.quantize_mx(T.wq[:, 256:512], T.ws[:, 256:512], T.w1t[:, 1024:2048]).then_inc(S.qw, 1)
+    V.quantize_mx(T.wq[:, 256:512], T.ws[:, 256:512], T.w1t[:, 1024:2048]).then_inc(S.qwb, 1)
     V.wait_ge(S.lw2, 16)
-    V.quantize_mx(T.wq[:, 512:640], T.ws[:, 512:640], T.w2t[:, :]).then_inc(S.qw, 1)
+    V.quantize_mx(T.wq[:, 512:640], T.ws[:, 512:640], T.w2t[:, :]).then_inc(S.qw2, 1)
     if window:
         if again:
             V.wait_ge(S.lx2, 16)
@@ -193,66 +242,80 @@ def rank_program(g, core, T, topo):
         for w, group in P["calls"][rank]:
             parts = []
             for _, h in group:
-                s0, _, _, a = P["slot"][rank, h]
-                d = 128 + s0
+                d = P["slot"][rank, h]
+                a = P["wide"][rank, h][2]
                 if scales:
                     parts.append((P["owner"][rank, h], T.bs[:, d:d + w], T.xs[:, a:a + w]))
                 else:
                     parts.append((P["owner"][rank, h], T.bq[:, d:d + w].bitcast(dt.uint8),
                                   T.xq[:, a:a + w].bitcast(dt.uint8)))
             left += send(parts, S.xin, S.dl, w if scales else 4 * w)
-    g.wait_ge(S.qw, 3)
     rid, pid, _ = topo.addr(cores[partner])
-    m = sum(1 << e for e in in_eng)
-    g.remote_dma(out_ap=T.pq[:, :].bitcast(dt.uint8), in_ap=T.wq[:, :].bitcast(dt.uint8), remote_sem=S.win,
-                 local_sem=S.wl, pid=pid, routing_id=rid, dma_engine_mask=m)
-    g.remote_dma(out_ap=T.ps[:, :], in_ap=T.ws[:, :], remote_sem=S.win, local_sem=S.wl, pid=pid, routing_id=rid,
-                 dma_engine_mask=m)
+    sent = {}
+    for a, b, ready, arrived, local, engs in ((0, 256, S.qwa, S.wina, "wl1", out_eng),
+                                              (256, 512, S.qwb, S.winb, "wl1", in_eng),
+                                              (512, 640, S.qw2, S.win2, "wl2", out_eng)):
+        g.wait_ge(ready, 1)
+        m = sum(1 << e for e in engs)
+        g.remote_dma(out_ap=T.pq[:, a:b].bitcast(dt.uint8), in_ap=T.wq[:, a:b].bitcast(dt.uint8), remote_sem=arrived,
+                     local_sem=S[local], pid=pid, routing_id=rid, dma_engine_mask=m)
+        g.remote_dma(out_ap=T.ps[:, a:b], in_ap=T.ws[:, a:b], remote_sem=arrived, local_sem=S[local], pid=pid,
+                     routing_id=rid, dma_engine_mask=m)
+        sent[local] = sent.get(local, 0) + 2 * len(engs)
 
     Y.wait_ge(S.dl, left)
-    Y.dma_start(T.s1t[:, :], T.s1[:, :]).then_inc(S.ls1, 16)
+    Y.wait_ge(S.wl1, sent["wl1"])
+    Y.dma_start(T.s1t[:, 0:1024], T.s1[:, 0:1024]).then_inc(S.ls1a, 16)
+    Y.dma_start(T.s1t[:, 1024:2048], T.s1[:, 1024:2048]).then_inc(S.ls1b, 16)
     Y.dma_start(T.s2t[:, :], T.s2[:, :]).then_inc(S.ls2, 16)
 
-    bank = lambda b, c=n: T.z[:, 512 * b:512 * b + c]
-    BQ, BS = T.bq[:, start:128 + L], T.bs[:, start:128 + L]
-    order = (0, 2, 1, 3)
+    def mm(wq, ws, i, bank, rq, rs, c, sem):
+        E.matmul_mx(T.z[:, 512 * bank:512 * bank + c], wq[:, 128 * i:128 * i + 128], ws[:, 128 * i:128 * i + 128], rq, rs,
+                    True, True).then_inc(sem, 1)
 
-    def firsts(wq, ws, name, rq, rs, c, banks):
-        for i in order:
-            E.matmul_mx(bank(banks[i], c), wq[:, 128 * i:128 * i + 128], ws[:, 128 * i:128 * i + 128], rq, rs, True,
-                        True).then_inc(S[name + "%d" % i], 1)
+    def act(q, dst, i, bank, src0, dst0, c, ready, done):
+        q.wait_ge(ready, 1)
+        out, src = dst[:, 4 * dst0 + i:4 * (dst0 + c):4], T.z[:, 512 * bank + src0:512 * bank + src0 + c]
+        if q is V:
+            q.tensor_scalar(out, src, 0.0, SCALE, AluOpType.max, AluOpType.mult).then_inc(done, 1)
+        else:
+            q.activation(out, src, ActivationFunctionType.Relu, scale=SCALE).then_inc(done, 1)
 
-    def acts(dst, name, c, banks, sv, sa):
-        for i in (0, 1):
-            V.wait_ge(S[name + "%d" % i], 1)
-            V.tensor_scalar(dst[:, i:4 * c:4], bank(banks[i], c), 0.0, SCALE, AluOpType.max,
-                            AluOpType.mult).then_inc(sv, 1)
-        for i in (2, 3):
-            A.wait_ge(S[name + "%d" % i], 1)
-            A.activation(dst[:, i:4 * c:4], bank(banks[i], c), ActivationFunctionType.Relu,
-                         scale=SCALE).then_inc(sa, 1)
-
-    OB, PB, KB = (0, 1, 2, 3), (4, 5, 6, 7), (1, 2, 3, 5)
-    E.wait_ge(S.qw, 3)
+    def view(e):
+        v, c = views[e][2], views[e][3]
+        return T.bq[:, v:v + c], T.bs[:, v:v + c], c
+    for ready in (S.qwa, S.qwb, S.qw2):
+        E.wait_ge(ready, 1)
     if window:
         E.wait_ge(S.qb, 1)
     E.wait_ge(S.xin, x_arrive)
-    firsts(T.wq, T.ws, "zo", BQ, BS, n, OB)
-    E.wait_ge(S.win, 2 * len(in_eng))
-    firsts(T.pq, T.ps, "zp", BQ, BS, n, PB)
+    rq, rs, no = view(rank)
+    for i in range(4):
+        mm(T.wq, T.ws, i, i, rq, rs, no, S["zo%d" % i])
+    rq, rs, np_ = view(partner)
+    for i in range(4):
+        if i == 0:
+            E.wait_ge(S.wina, 2 * len(out_eng))
+        if i == 2:
+            E.wait_ge(S.winb, 2 * len(in_eng))
+        mm(T.pq, T.ps, i, 4 + i, rq, rs, np_, S["zp%d" % i])
     E.wait_ge(S.qho, 1)
-    E.matmul_mx(bank(0), T.wq[:, 512:640], T.ws[:, 512:640], T.hoq[:, 0:n], T.hos[:, 0:n], True, True).then_inc(S.po, 1)
+    mm(T.wq, T.ws, 4, 0, T.hoq[:, 0:no], T.hos[:, 0:no], no, S.po)
+    E.wait_ge(S.win2, 2 * len(out_eng))
     E.wait_ge(S.qhp, 1)
-    E.matmul_mx(bank(4), T.pq[:, 512:640], T.ps[:, 512:640], T.hpq[:, 0:n], T.hps[:, 0:n], True, True).then_inc(S.pp, 1)
+    mm(T.pq, T.ps, 4, 4, T.hpq[:, 0:np_], T.hps[:, 0:np_], np_, S.pp)
 
-    acts(T.ho, "zo", n, OB, S.aov, S.aos)
-    V.wait_ge(S.aov, 2)
-    V.wait_ge(S.aos, 2)
-    V.quantize_mx(T.hoq[:, 0:n], T.hos[:, 0:n], T.ho[:, 0:4 * n]).then_inc(S.qho, 1)
-    acts(T.hp, "zp", n, PB, S.apv, S.aps)
-    V.wait_ge(S.apv, 2)
-    V.wait_ge(S.aps, 2)
-    V.quantize_mx(T.hpq[:, 0:n], T.hps[:, 0:n], T.hp[:, 0:4 * n]).then_inc(S.qhp, 1)
+    if fills:
+        V.wait_ge(S.mh, fills)
+        A.wait_ge(S.mh, fills)
+    for e, dst, dq, ds, b0, name, av, aa, done in ((rank, T.ho, T.hoq, T.hos, 0, "zo", S.aov, S.aos, S.qho),
+                                                   (partner, T.hp, T.hpq, T.hps, 4, "zp", S.apv, S.aps, S.qhp)):
+        lo, k, v, c = views[e]
+        for i in range(4):
+            act(A if i % 2 else V, dst, i, b0 + i, lo - v, lo - v, k, S[name + "%d" % i], aa if i % 2 else av)
+        V.wait_ge(av, 2)
+        V.wait_ge(aa, 2)
+        V.quantize_mx(dq[:, 0:c], ds[:, 0:c], dst[:, 0:4 * c]).then_inc(done, 1)
 
     groups = return_groups(rank)
     assert len(groups) <= RG
@@ -271,17 +334,13 @@ def rank_program(g, core, T, topo):
             c = cnt[j][e]
             if c == 0:
                 continue
-            lead = off[j][e] - P["run"][j, home][0]
+            src = P["where"][rank, j, e] - views[e][2]
             if gi is None:
-                src = 128 - own + lead - start
-                dst = T.land[:, off[j][e]:off[j][e] + c]
-                sem = S.ol
+                dst, sem = T.land[:, off[j][e]:off[j][e] + c], S.ol
                 own_need += 1
             else:
-                s0, _, skip, _ = P["slot"][j, home]
-                src = 128 + s0 + skip + lead - start
-                dst = T.ret[:, p + lead:p + lead + c]
-                sem = S["r%d" % gi]
+                lead = off[j][e] - P["run"][j, home][0]
+                dst, sem = T.ret[:, p + lead:p + lead + c], S["r%d" % gi]
                 need[gi] += 1
             if e == rank:
                 A.activation(dst, T.z[:, src:src + c], ActivationFunctionType.Copy).then_inc(sem, 1)
@@ -298,27 +357,35 @@ def rank_program(g, core, T, topo):
             pos += w
         back += send(parts, S.pin, S.rl, 4 * w)
 
-    V.wait_ge(S.ls1, 16)
-    V.quantize_mx(T.sq[:, 0:512], T.ss[:, 0:512], T.s1t[:, :]).then_inc(S.qs, 1)
+    V.wait_ge(S.ls1a, 16)
+    V.quantize_mx(T.sq[:, 0:256], T.ss[:, 0:256], T.s1t[:, 0:1024]).then_inc(S.qsa, 1)
+    V.wait_ge(S.ls1b, 16)
+    V.quantize_mx(T.sq[:, 256:512], T.ss[:, 256:512], T.s1t[:, 1024:2048]).then_inc(S.qsb, 1)
     V.wait_ge(S.ls2, 16)
-    V.quantize_mx(T.sq[:, 512:640], T.ss[:, 512:640], T.s2t[:, :]).then_inc(S.qs, 1)
-    E.wait_ge(S.qs, 2)
+    V.quantize_mx(T.sq[:, 512:640], T.ss[:, 512:640], T.s2t[:, :]).then_inc(S.qs2, 1)
     E.wait_ge(S.qx, 1)
-    firsts(T.sq, T.ss, "zk", T.xq[:, :], T.xs[:, :], nc, KB)
-    acts(T.kt, "zk", nc, KB, S.akv, S.aks)
-    V.wait_ge(S.akv, 2)
-    V.wait_ge(S.aks, 2)
+    KB = (1, 2, 3, 5)
+    for i in range(4):
+        if i % 2 == 0:
+            E.wait_ge(S.qsa if i == 0 else S.qsb, 1)
+        mm(T.sq, T.ss, i, KB[i], T.xq[:, :], T.xs[:, :], nc, S["zk%d" % i])
+    for i in range(4):
+        act(A if i < 3 else V, T.kt, i, KB[i], 0, 0, nc, S["zk%d" % i], S.aks if i < 3 else S.akv)
+    V.wait_ge(S.akv, 1)
+    V.wait_ge(S.aks, 3)
     V.quantize_mx(T.kq[:, :], T.ks[:, :], T.kt[:, :]).then_inc(S.qk, 1)
+    E.wait_ge(S.qs2, 1)
     E.wait_ge(S.qk, 1)
-    E.matmul_mx(bank(6, nc), T.sq[:, 512:640], T.ss[:, 512:640], T.kq[:, :], T.ks[:, :], True, True).then_inc(S.uu, 1)
+    mm(T.sq, T.ss, 4, 6, T.kq[:, :], T.ks[:, :], nc, S.uu)
 
     V.wait_ge(S.uu, 1)
     if own_need:
         V.wait_ge(S.ol, own_need)
     V.wait_ge(S.pin, p_arrive)
-    V.tensor_tensor(T.ysb[:, :], T.land[:, :], bank(6, nc), AluOpType.add).then_inc(S.yv, 1)
+    V.tensor_tensor(T.ysb[:, :], T.land[:, :], T.z[:, 3072:3072 + nc], AluOpType.add).then_inc(S.yv, 1)
     Y.wait_ge(S.yv, 1)
     Y.dma_start(T.y[:, :], T.ysb[:, :]).then_inc(S.sy, 16)
     Y.wait_ge(S.sy, 16)
-    g.wait_ge(S.wl, 2 * len(in_eng))
+    g.wait_ge(S.wl1, sent["wl1"])
+    g.wait_ge(S.wl2, sent["wl2"])
     g.wait_ge(S.rl, back)

from concourse.bass import DstId, RemoteDMATransfer
from concourse.mybir import dt, AluOpType, ActivationFunctionType

NB = 352
SCALE = 0.019
SCRATCH = {
    "xt": ("sbuf", [128, 1024], "bfloat16"),
    "w1t": ("sbuf", [128, 2048], "bfloat16"),
    "w2t": ("sbuf", [128, 512], "bfloat16"),
    "s1t": ("sbuf", [128, 2048], "bfloat16"),
    "s2t": ("sbuf", [128, 512], "bfloat16"),
    "xq": ("sbuf", [128, 128], "float8_e4m3fn_x4"),
    "xs": ("sbuf", [128, 128], "uint8"),
    "wq": ("sbuf", [128, 640], "float8_e4m3fn_x4"),
    "ws": ("sbuf", [128, 640], "uint8"),
    "pq": ("sbuf", [128, 640], "float8_e4m3fn_x4"),
    "ps": ("sbuf", [128, 640], "uint8"),
    "sq": ("sbuf", [128, 640], "float8_e4m3fn_x4"),
    "ss": ("sbuf", [128, 640], "uint8"),
    "bq": ("sbuf", [128, NB], "float8_e4m3fn_x4"),
    "bs": ("sbuf", [128, NB], "uint8"),
    "ho": ("sbuf", [128, 4 * NB], "bfloat16"),
    "hp": ("sbuf", [128, 4 * NB], "bfloat16"),
    "hoq": ("sbuf", [128, NB], "float8_e4m3fn_x4"),
    "hos": ("sbuf", [128, NB], "uint8"),
    "hpq": ("sbuf", [128, NB], "float8_e4m3fn_x4"),
    "hps": ("sbuf", [128, NB], "uint8"),
    "kt": ("sbuf", [128, 512], "bfloat16"),
    "kq": ("sbuf", [128, 128], "float8_e4m3fn_x4"),
    "ks": ("sbuf", [128, 128], "uint8"),
    "ret": ("sbuf", [128, NB], "float32"),
    "land": ("sbuf", [128, 128], "float32"),
    "ysb": ("sbuf", [128, 128], "float32"),
    "z": ("psum", [128, 4096], "float32"),
}
RG = 8
SEMAPHORES = (["lx", "lx2", "xgo", "lwa", "lwb", "lw2", "ls1a", "ls1b", "ls2", "mh", "qx", "qb", "qwa", "qwb", "qw2",
               "qsa", "qsb", "qs2", "xin", "wina", "winb", "win2", "dl", "wl1", "wl2",
               "rl", "aov", "aos", "apv", "aps", "qho", "qhp", "po", "pp", "ol", "akv", "aks", "qk", "uu", "pin",
               "yv", "sy"] + ["zo%d" % i for i in range(4)] + ["zp%d" % i for i in range(4)]
              + ["zk%d" % i for i in range(4)] + ["r%d" % i for i in range(RG)])


def share(n, t):
    out = [n]
    while len(out) < t:
        out.sort(reverse=True)
        out = [out[0] // 2, out[0] // 2] + out[1:]
    return sorted(out)


def deal(load, t, cost):
    lists = []
    left = sorted(load, key=lambda e: (load[e], e))
    for k in share(len(left), t):
        pick = left[:k]
        left = left[k:]
        for e in pick:
            load[e] += cost / k
        lists.append(pick)
    return lists


def row_cost(width_bytes):
    return 128.0 * (8.0 + 0.04 * width_bytes)


def classes(runs, ne, most=3):
    runs = sorted(runs)
    best = None
    m = len(runs)
    for cuts in range(1 << (m - 1)):
        edge = [0] + [i + 1 for i in range(m - 1) if (cuts >> i) & 1] + [m]
        calls = [(runs[b - 1][0], runs[a:b]) for a, b in zip(edge, edge[1:])]
        if len(calls) > most or max(len(c[1]) for c in calls) > ne:
            continue
        load = {e: 0.0 for e in range(ne)}
        for size in (4, 1):
            for w, group in calls:
                deal(load, len(group), row_cost(size * w))
        cost = max(load.values()) + 10.0 * sum(w - q[0] for w, group in calls for q in group)
        if best is None or cost < best[0]:
            best = (cost, calls)
    return best[1]


def make_plan(cores, cnt, topo):
    n = len(cores)
    nc = sum(cnt[0])
    off = [[sum(c[:e]) for e in range(n + 1)] for c in cnt]
    pair = {}
    for r in range(n):
        pair[r] = [q for q in range(n) if topo.chip(cores[q]) == topo.chip(cores[r])]
    heads = sorted(set(pair[r][0] for r in range(n)))
    owner = {}
    for j in range(n):
        for h in heads:
            owner[j, h] = [q for q in pair[h] if topo.die(cores[q]) == topo.die(cores[j])][0]
    run = {(j, h): (off[j][h], off[j][pair[h][-1] + 1]) for j in range(n) for h in heads}
    calls = {}
    wide = {}
    for j in range(n):
        rs = [(run[j, h][1] - run[j, h][0], h) for h in heads if h != pair[j][0] and run[j, h][1] > run[j, h][0]]
        calls[j] = classes(rs, 8)
        for w, group in calls[j]:
            for _, h in group:
                a = min(run[j, h][0], nc - w)
                wide[j, h] = (w, run[j, h][0] - a, a)
    slot = {}
    where = {}
    end = {}
    for r in range(n):
        h, o = pair[r]
        src = [j for j in range(n) if (j, h) in wide and owner[j, h] == r]
        first = [j for j in src if cnt[j][o] == 0]
        second = [j for j in src if cnt[j][h] == 0]
        both = sorted([j for j in src if cnt[j][h] and cnt[j][o]], key=lambda j: cnt[j][o] - cnt[j][h])
        size = lambda g: sum(wide[j, h][0] for j in g)
        if cnt[r][h] and cnt[r][o]:
            seq = both + sorted([first, second], key=size)[0] + sorted([first, second], key=size)[1]
        elif cnt[r][o]:
            seq = second + both[::-1] + first
        else:
            seq = first + both + second
        pos = 128
        for e in (h, o):
            where[r, r, e] = 128 - (run[r, h][1] - off[r][e])
        for j in seq:
            slot[j, h] = pos
            for e in (h, o):
                where[r, j, e] = pos + wide[j, h][1] + off[j][e] - off[j][h]
            pos += wide[j, h][0]
        end[r] = pos
    return {"off": off, "pair": pair, "owner": owner, "run": run, "calls": calls, "wide": wide, "slot": slot,
            "where": where, "end": end, "nc": nc}


def rank_program(g, core, T, topo):
    rank = T.rank_of(core)
    if rank is None:
        return
    cores, cnt = T.cores, T.tables["CNT"]
    P = make_plan(cores, cnt, topo)
    off, nc = P["off"], P["nc"]
    home = P["pair"][rank][0]
    partner = [q for q in P["pair"][rank] if q != rank][0]
    S = T.sem
    V, A, E, Y = g.vector, g.scalar, g.tensor, g.sync
    bits = lambda m: [i for i in range(16) if (m >> i) & 1]
    far = [q for q in range(len(cores)) if q not in P["pair"][rank] and topo.die(cores[q]) == topo.die(core)]
    for q in far + [partner]:
        assert topo.may_write(core, cores[q])
    out_eng = bits(topo.mask(core, cores[far[0]]))
    in_eng = [e for e in bits(topo.mask(core, cores[partner])) if e not in out_eng]
    assert len(out_eng) == 8
    load = {e: 0.0 for e in out_eng}

    def send(parts, remote_sem, local_sem, width_bytes):
        masks = [sum(1 << e for e in l) for l in deal(load, len(parts), row_cost(width_bytes))]
        if len(parts) == 1:
            q, o, i = parts[0]
            rid, pid, _ = topo.addr(cores[q])
            g.remote_dma(out_ap=o, in_ap=i, remote_sem=remote_sem, local_sem=local_sem, pid=pid, routing_id=rid,
                         dma_engine_mask=masks[0])
        else:
            tr = []
            for (q, o, i), m in zip(parts, masks):
                rid, pid, _ = topo.addr(cores[q])
                tr.append(RemoteDMATransfer(dst_ids=[DstId(rid=rid, pnc=pid)], dma_engine_mask=m, remote_sem=remote_sem,
                                            src=i, dst=o))
            g.remote_dma_fused(tr, local_sem=local_sem)
        return sum(len(bits(m)) for m in masks)

    def engines_in(groups):
        out = {}
        for group in groups:
            for key, k in zip(group, share(len(out_eng), len(group))):
                out[key] = out.get(key, 0) + k
        return out

    def return_groups(r):
        h = P["pair"][r][0]
        other = [q for q in P["pair"][r] if q != r][0]
        by = {}
        for j in range(len(cores)):
            if (j, h) in P["slot"] and P["owner"][j, h] == r:
                by.setdefault((cnt[j][other] > 0, P["run"][j, h][1] - P["run"][j, h][0]), []).append(j)
        keys = sorted(by, key=lambda k: (k[0], -len(by[k]), -k[1]))
        single = [k for k in keys if k[0] and len(by[k]) == 1]
        if single:
            keys.remove(single[0])
            keys.insert(len([k for k in keys if not k[0]]), single[0])
        return [(k[1], by[k]) for k in keys]

    x_arrive = sum(2 * engines_in([[h for _, h in gr] for _, gr in P["calls"][j]]).get(home, 0) for j in far)
    p_arrive = sum(engines_in([js for _, js in return_groups(r)]).get(rank, 0) for r in far)

    own_b = P["run"][rank, home][1]
    end = P["end"][rank]
    assert end <= NB
    views = {}
    for e in (rank, partner):
        cols = [(P["where"][rank, j, e], cnt[j][e]) for j in range(len(cores)) if (rank, j, e) in P["where"] and cnt[j][e]]
        lo = min(c for c, _ in cols)
        hi = max(c + k for c, k in cols)
        v = lo if lo + 128 <= end else min(lo, end - 128)
        views[e] = (lo, hi - lo, v, max(128, hi - v))
    window = min(views[e][2] for e in views) < 128

    Y.dma_start(T.xt[:, 512:1024], T.x[:, :]).then_inc(S.lx, 16)
    Y.sem_inc(S.xgo, 1)
    Y.dma_start(T.w1t[:, 0:1024], T.w1[:, 0:1024]).then_inc(S.lwa, 16)
    A.wait_ge(S.xgo, 1)
    A.dma_start(T.w1t[:, 1024:2048], T.w1[:, 1024:2048]).then_inc(S.lwb, 16)
    A.dma_start(T.w2t[:, :], T.w2[:, :]).then_inc(S.lw2, 16)
    again = window and own_b < nc
    if again:
        A.dma_start(T.xt[:, 4 * own_b:512], T.x[:, 4 * own_b:512]).then_inc(S.lx2, 16)

    fills = 0
    for e, t in ((rank, T.ho), (partner, T.hp)):
        if views[e][1] < views[e][3]:
            V.memset(t[:, 0:4 * views[e][3]], 0.0).then_inc(S.mh, 1)
            fills += 1

    V.wait_ge(S.lx, 16)
    V.quantize_mx(T.xq[:, :], T.xs[:, :], T.xt[:, 512:1024]).then_inc(S.qx, 1)
    V.wait_ge(S.lwa, 16)
    V.quantize_mx(T.wq[:, 0:256], T.ws[:, 0:256], T.w1t[:, 0:1024]).then_inc(S.qwa, 1)
    V.wait_ge(S.lwb, 16)
    V.quantize_mx(T.wq[:, 256:512], T.ws[:, 256:512], T.w1t[:, 1024:2048]).then_inc(S.qwb, 1)
    V.wait_ge(S.lw2, 16)
    V.quantize_mx(T.wq[:, 512:640], T.ws[:, 512:640], T.w2t[:, :]).then_inc(S.qw2, 1)
    if window:
        if again:
            V.wait_ge(S.lx2, 16)
        V.quantize_mx(T.bq[:, 0:128], T.bs[:, 0:128], T.xt[:, 4 * own_b:4 * own_b + 512]).then_inc(S.qb, 1)

    g.wait_ge(S.qx, 1)
    left = 0
    for scales in (False, True):
        for w, group in P["calls"][rank]:
            parts = []
            for _, h in group:
                d = P["slot"][rank, h]
                a = P["wide"][rank, h][2]
                if scales:
                    parts.append((P["owner"][rank, h], T.bs[:, d:d + w], T.xs[:, a:a + w]))
                else:
                    parts.append((P["owner"][rank, h], T.bq[:, d:d + w].bitcast(dt.uint8),
                                  T.xq[:, a:a + w].bitcast(dt.uint8)))
            left += send(parts, S.xin, S.dl, w if scales else 4 * w)
    rid, pid, _ = topo.addr(cores[partner])
    sent = {}
    for a, b, ready, arrived, local, engs in ((0, 256, S.qwa, S.wina, "wl1", out_eng),
                                              (256, 512, S.qwb, S.winb, "wl1", in_eng),
                                              (512, 640, S.qw2, S.win2, "wl2", out_eng)):
        g.wait_ge(ready, 1)
        m = sum(1 << e for e in engs)
        g.remote_dma(out_ap=T.pq[:, a:b].bitcast(dt.uint8), in_ap=T.wq[:, a:b].bitcast(dt.uint8), remote_sem=arrived,
                     local_sem=S[local], pid=pid, routing_id=rid, dma_engine_mask=m)
        g.remote_dma(out_ap=T.ps[:, a:b], in_ap=T.ws[:, a:b], remote_sem=arrived, local_sem=S[local], pid=pid,
                     routing_id=rid, dma_engine_mask=m)
        sent[local] = sent.get(local, 0) + 2 * len(engs)

    Y.wait_ge(S.dl, left)
    Y.wait_ge(S.wl1, sent["wl1"])
    Y.dma_start(T.s1t[:, 0:1024], T.s1[:, 0:1024]).then_inc(S.ls1a, 16)
    Y.dma_start(T.s1t[:, 1024:2048], T.s1[:, 1024:2048]).then_inc(S.ls1b, 16)
    Y.dma_start(T.s2t[:, :], T.s2[:, :]).then_inc(S.ls2, 16)

    def mm(wq, ws, i, bank, rq, rs, c, sem):
        E.matmul_mx(T.z[:, 512 * bank:512 * bank + c], wq[:, 128 * i:128 * i + 128], ws[:, 128 * i:128 * i + 128], rq, rs,
                    True, True).then_inc(sem, 1)

    def act(q, dst, i, bank, src0, dst0, c, ready, done):
        q.wait_ge(ready, 1)
        out, src = dst[:, 4 * dst0 + i:4 * (dst0 + c):4], T.z[:, 512 * bank + src0:512 * bank + src0 + c]
        if q is V:
            q.tensor_scalar(out, src, 0.0, SCALE, AluOpType.max, AluOpType.mult).then_inc(done, 1)
        else:
            q.activation(out, src, ActivationFunctionType.Relu, scale=SCALE).then_inc(done, 1)

    def view(e):
        v, c = views[e][2], views[e][3]
        return T.bq[:, v:v + c], T.bs[:, v:v + c], c
    for ready in (S.qwa, S.qwb, S.qw2):
        E.wait_ge(ready, 1)
    if window:
        E.wait_ge(S.qb, 1)
    E.wait_ge(S.xin, x_arrive)
    rq, rs, no = view(rank)
    for i in range(4):
        mm(T.wq, T.ws, i, i, rq, rs, no, S["zo%d" % i])
    rq, rs, np_ = view(partner)
    for i in range(4):
        if i == 0:
            E.wait_ge(S.wina, 2 * len(out_eng))
        if i == 2:
            E.wait_ge(S.winb, 2 * len(in_eng))
        mm(T.pq, T.ps, i, 4 + i, rq, rs, np_, S["zp%d" % i])
    E.wait_ge(S.qho, 1)
    mm(T.wq, T.ws, 4, 0, T.hoq[:, 0:no], T.hos[:, 0:no], no, S.po)
    E.wait_ge(S.win2, 2 * len(out_eng))
    E.wait_ge(S.qhp, 1)
    mm(T.pq, T.ps, 4, 4, T.hpq[:, 0:np_], T.hps[:, 0:np_], np_, S.pp)

    if fills:
        V.wait_ge(S.mh, fills)
        A.wait_ge(S.mh, fills)
    for e, dst, dq, ds, b0, name, av, aa, done in ((rank, T.ho, T.hoq, T.hos, 0, "zo", S.aov, S.aos, S.qho),
                                                   (partner, T.hp, T.hpq, T.hps, 4, "zp", S.apv, S.aps, S.qhp)):
        lo, k, v, c = views[e]
        for i in range(4):
            act(A if i % 2 else V, dst, i, b0 + i, lo - v, lo - v, k, S[name + "%d" % i], aa if i % 2 else av)
        V.wait_ge(av, 2)
        V.wait_ge(aa, 2)
        V.quantize_mx(dq[:, 0:c], ds[:, 0:c], dst[:, 0:4 * c]).then_inc(done, 1)

    groups = return_groups(rank)
    assert len(groups) <= RG
    jobs = []
    pos = 0
    for gi, (w, js) in enumerate(groups):
        for j in js:
            jobs.append((j, pos, gi))
            pos += w
    need = [0] * len(groups)
    own_need = 0
    A.wait_ge(S.po, 1)
    V.wait_ge(S.pp, 1)
    for e in (rank, partner):
        for j, p, gi in jobs + [(rank, None, None)]:
            c = cnt[j][e]
            if c == 0:
                continue
            src = P["where"][rank, j, e] - views[e][2]
            if gi is None:
                dst, sem = T.land[:, off[j][e]:off[j][e] + c], S.ol
                own_need += 1
            else:
                lead = off[j][e] - P["run"][j, home][0]
                dst, sem = T.ret[:, p + lead:p + lead + c], S["r%d" % gi]
                need[gi] += 1
            if e == rank:
                A.activation(dst, T.z[:, src:src + c], ActivationFunctionType.Copy).then_inc(sem, 1)
            else:
                V.tensor_copy(dst, T.z[:, 2048 + src:2048 + src + c]).then_inc(sem, 1)
    back = 0
    pos = 0
    for gi, (w, js) in enumerate(groups):
        g.wait_ge(S["r%d" % gi], need[gi])
        parts = []
        for j in js:
            a, b = P["run"][j, home]
            parts.append((j, T.land[:, a:b], T.ret[:, pos:pos + w]))
            pos += w
        back += send(parts, S.pin, S.rl, 4 * w)

    V.wait_ge(S.ls1a, 16)
    V.quantize_mx(T.sq[:, 0:256], T.ss[:, 0:256], T.s1t[:, 0:1024]).then_inc(S.qsa, 1)
    V.wait_ge(S.ls1b, 16)
    V.quantize_mx(T.sq[:, 256:512], T.ss[:, 256:512], T.s1t[:, 1024:2048]).then_inc(S.qsb, 1)
    V.wait_ge(S.ls2, 16)
    V.quantize_mx(T.sq[:, 512:640], T.ss[:, 512:640], T.s2t[:, :]).then_inc(S.qs2, 1)
    E.wait_ge(S.qx, 1)
    KB = (1, 2, 3, 5)
    for i in range(4):
        if i % 2 == 0:
            E.wait_ge(S.qsa if i == 0 else S.qsb, 1)
        mm(T.sq, T.ss, i, KB[i], T.xq[:, :], T.xs[:, :], nc, S["zk%d" % i])
    for i in range(4):
        act(A if i < 3 else V, T.kt, i, KB[i], 0, 0, nc, S["zk%d" % i], S.aks if i < 3 else S.akv)
    V.wait_ge(S.akv, 1)
    V.wait_ge(S.aks, 3)
    V.quantize_mx(T.kq[:, :], T.ks[:, :], T.kt[:, :]).then_inc(S.qk, 1)
    E.wait_ge(S.qs2, 1)
    E.wait_ge(S.qk, 1)
    mm(T.sq, T.ss, 4, 6, T.kq[:, :], T.ks[:, :], nc, S.uu)

    V.wait_ge(S.uu, 1)
    if own_need:
        V.wait_ge(S.ol, own_need)
    V.wait_ge(S.pin, p_arrive)
    V.tensor_tensor(T.ysb[:, :], T.land[:, :], T.z[:, 3072:3072 + nc], AluOpType.add).then_inc(S.yv, 1)
    Y.wait_ge(S.yv, 1)
    Y.dma_start(T.y[:, :], T.ysb[:, :]).then_inc(S.sy, 16)
    Y.wait_ge(S.sy, 16)
    g.wait_ge(S.wl1, sent["wl1"])
    g.wait_ge(S.wl2, sent["wl2"])
    g.wait_ge(S.rl, back)
